import numpy as np
import ml_dtypes


def mxq(x, axis, fmt="e4m3"):
    dtype, down = {"e4m3": (ml_dtypes.float8_e4m3fn, 7), "e5m2": (ml_dtypes.float8_e5m2, 14)}[fmt]
    v = np.moveaxis(np.asarray(x, np.float32).astype(ml_dtypes.bfloat16).astype(np.float64), axis, -1)
    blocks = v.reshape(v.shape[:-1] + (-1, 32))
    amax = np.abs(blocks).max(-1, keepdims=True)
    byte = np.maximum(np.where(amax > 0, np.frexp(amax)[1] - 1 + 127, 0) - down, 1)
    scale = np.exp2(byte - 127.0)
    codes = (blocks / scale).astype(np.float32).astype(dtype).astype(np.float64)
    return np.moveaxis((codes * scale).reshape(v.shape), -1, axis)


WIDE = False


def mx_kscale(k):
    if not WIDE:
        return np.ones(k)
    levels = np.array([10, -10, 5, -5, 0])
    if k % 512:
        return np.exp2(np.random.permutation(np.resize(levels, k // 32))).repeat(32)
    a = np.empty((k // 512, 16))
    for p in range(k // 512):
        a[p, :8] = np.random.permutation(np.resize(levels, 8))
        for g in range(8):
            far = levels[np.abs(levels - a[p, g]) >= 10]
            a[p, g + 8] = far[np.random.randint(len(far))]
    return np.exp2(a.ravel()).repeat(32)


def f64(x):
    return np.asarray(x).astype(np.float64)


def striped(idx):
    return np.tile(np.asarray(idx).reshape(-1, 16).T, (8, 1)).astype(np.uint16)


def unstriped(offs):
    return offs[:16].T.reshape(-1).astype(np.int64)


E2M1 = np.array([0.0, 0.5, 1.0, 1.5, 2.0, 3.0, 4.0, 6.0, -0.0, -0.5, -1.0, -1.5, -2.0, -3.0, -4.0, -6.0])


def pack_weight(w, fmt):
    k, n = w.shape
    w = f64(np.asarray(w, np.float32).astype(ml_dtypes.bfloat16)).reshape(k // 32, 32, n)
    amax = np.abs(w).max(1)
    if fmt == "e4m3":
        byte = np.frexp(amax)[1] - 1 + 127 - 7
    else:
        mant, ex = np.frexp(amax / 6.0)
        byte = np.where(mant > 0.5, ex, ex - 1) + 127
    byte = np.clip(np.where(amax > 0, byte, 1), 1, 254)
    scaled = (w * np.exp2(127.0 - byte)[:, None, :]).reshape(k, n).astype(np.float32)
    by_word = np.ascontiguousarray(scaled.reshape(k // 512, 128, 4, n).transpose(0, 1, 3, 2))
    if fmt == "e4m3":
        words = by_word.astype(ml_dtypes.float8_e4m3fn).view(np.uint8)
    else:
        c = by_word.astype(ml_dtypes.float4_e2m1fn).view(np.uint8) & 0xF
        words = (c[..., 0::2] | (c[..., 1::2] << 4)).reshape(k // 512, 128, 2 * n)
    return np.ascontiguousarray(words), np.ascontiguousarray(byte.astype(np.uint8).reshape(k // 512, 16, n))


def unpack_weight(words, scales, fmt):
    g, _, n = scales.shape
    words = np.ascontiguousarray(words).reshape(g, 128, n, -1)
    if fmt == "e4m3":
        vals = words.view(ml_dtypes.float8_e4m3fn).astype(np.float64)
    else:
        nib = np.empty((g, 128, n, 4), np.uint8)
        nib[..., 0::2] = words & 0xF
        nib[..., 1::2] = words >> 4
        vals = E2M1[nib]
    vals = vals * np.repeat(np.exp2(scales.astype(np.float64) - 127.0), 8, axis=1)[..., None]
    return vals.transpose(0, 1, 3, 2).reshape(g * 512, n)


def sigmoid(v):
    return 1.0 / (1.0 + np.exp(-v))


def bf(x):
    return np.asarray(x, np.float32).astype(ml_dtypes.bfloat16)


def planes(Y):
    r, m = Y.shape
    b = f64(bf(Y)).reshape(r // 32, 32, m)
    amax = np.abs(b).max(1)
    byte = np.clip(np.where(amax > 0, np.frexp(amax)[1] - 1 + 127 - 7, 1), 1, 254)
    codes = (b * np.exp2(127.0 - byte)[:, None, :]).reshape(r, m).astype(np.float32).astype(ml_dtypes.float8_e4m3fn).view(np.uint8)
    words = codes.reshape(r // 512, 128, 4, m).transpose(0, 1, 3, 2)
    return np.ascontiguousarray(words), np.ascontiguousarray(byte.astype(np.uint8).reshape(r // 512, 16, m))


K, T, J, N = 1024, 1024, 512, 512


def setup_inputs():
    n = np.random.standard_normal
    idx = np.random.permutation(T)[:J]
    idx2 = np.random.permutation(T)[:J]
    fk = mx_kscale(K)
    wap = pack_weight(n((K, N)) * 1 / np.sqrt(K) * fk[:, None], "e2m1")
    wbp = pack_weight(n((K, N)) * 1 / np.sqrt(K) * fk[:, None], "e4m3")
    return {
        "xt": (n((K, T)) / fk[:, None]).astype(np.float32),
        "wa_words": wap[0],
        "wa_scales": wap[1],
        "wb_words": wbp[0],
        "wb_scales": wbp[1],
        "res": (1.0 * n((N, T))).astype(np.float32),
        "offs": striped(idx),
        "offs2": striped(idx2),
    }


def reference(xt, wa_words, wa_scales, wb_words, wb_scales, res, offs, offs2):
    idx = unstriped(offs)
    idx2 = unstriped(offs2)
    wau = unpack_weight(wa_words, wa_scales, "e2m1")
    wbu = unpack_weight(wb_words, wb_scales, "e4m3")
    xtidxq = mxq(f64(xt)[:, idx], 0, "e4m3")
    a = wau.T @ xtidxq
    xtidx2q = mxq(f64(xt)[:, idx2], 0, "e4m3")
    b = wbu.T @ xtidx2q
    d = a * sigmoid(b)
    dp = np.zeros((N, T))
    dp[:, idx] = d
    y = dp + 0.4 * f64(res)
    words, scales = planes(y)
    return y, words, scales

@@ -1,0 +1,278 @@
+from contextlib import ExitStack
+
+import concourse.mybir as mybir
+
+K, T, J, N = 1024, 1024, 512, 512
+FLOPS = 2 * 2 * K * N * J
+
+F32 = mybir.dt.float32
+BF16 = mybir.dt.bfloat16
+I32 = mybir.dt.int32
+U32 = mybir.dt.uint32
+U16 = mybir.dt.uint16
+U8 = mybir.dt.uint8
+FP8X4 = mybir.dt.float8_e4m3fn_x4
+FP4X4 = mybir.dt.float4_e2m1fn_x4
+COPY = mybir.ActivationFunctionType.Copy
+SIGMOID = mybir.ActivationFunctionType.Sigmoid
+MULT = mybir.AluOpType.mult
+ADD = mybir.AluOpType.add
+
+P = 128
+PASSES = 2
+HALF_T = T // 2
+HALF_J = J // 2
+CHUNK = 256
+
+
+def tile_moe_one_expert_gates_another_pl_kernel(
+    tc, xt, wa_words, wa_scales, wb_words, wb_scales, res, offs, offs2, out_0, out_1, out_2
+):
+    nc = tc.nc
+    with ExitStack() as ctx:
+        keep = ctx.enter_context(tc.tile_pool(name="keep", bufs=1))
+        psum = ctx.enter_context(tc.psum_pool(name="psum", bufs=1))
+
+        def sbuf(name, shape, dtype):
+            return keep.tile(shape, dtype, name=name, align_bytes=64)
+
+        list_a = sbuf("list_a", [P, J // 16], U16)
+        list_b = sbuf("list_b", [P, J // 16], U16)
+        lists = {"a": list_a, "b": list_b}
+
+        x_rows = xt.rearrange("(g p u e) t -> g u p e t", g=PASSES, u=2, e=2)
+        raw = {}
+        for g in range(PASSES):
+            for u in range(2):
+                for h in range(2):
+                    raw[g, u, h] = sbuf("raw%d%d%d" % (g, u, h), [P, 2, HALF_T], F32)
+                    nc.sync.dma_start(out=raw[g, u, h][:], in_=x_rows[g, u, :, :, h * HALF_T : (h + 1) * HALF_T])
+                if (g, u) == (0, 0):
+                    nc.sync.dma_start(list_b[:], offs2)
+                    nc.sync.dma_start(list_a[:], offs)
+
+        wa_raw = sbuf("wa_raw", [P, PASSES, 2 * N], U8)
+        wb_raw = sbuf("wb_raw", [P, PASSES, N], I32)
+        nc.sync.dma_start(out=wa_raw[:].bitcast(I32), in_=wa_words.bitcast(I32).rearrange("g p w -> p g w"))
+        nc.sync.dma_start(
+            out=wb_raw[:], in_=wb_words.rearrange("g p n r -> g p (n r)").bitcast(I32).rearrange("g p w -> p g w")
+        )
+        ws_raw = sbuf("ws_raw", [P, PASSES, N], U8)
+        nc.vector.memset(ws_raw[:].bitcast(I32), 0)
+        for first_row, scales in ((0, wa_scales), (4, wb_scales)):
+            rows = scales.bitcast(I32).rearrange("g (q r) w -> q r g w", r=4)
+            for q in range(4):
+                row = 32 * q + first_row
+                nc.sync.dma_start(out=ws_raw[row : row + 4].bitcast(I32), in_=rows[q])
+
+        res_rows = res.rearrange("(p r) t -> r p t", r=4)
+        out_rows = out_0.rearrange("(p r) t -> r p t", r=4)
+        out_pairs = out_0.rearrange("(p u e) t -> u p e t", u=2, e=2)
+        res_sb = []
+        for r in range(4):
+            res_sb.append(sbuf("res%d" % r, [P, T], F32))
+            nc.sync.dma_start(out=res_sb[r][:], in_=res_rows[r])
+
+        warm_in = sbuf("warm_in", [P, 1], F32)
+        warm_out = sbuf("warm_out", [P, 1], F32)
+        nc.vector.memset(warm_in[:], 0.0)
+        nc.scalar.activation(warm_out[:], warm_in[:], SIGMOID)
+        placed = []
+        for r in range(4):
+            placed.append(sbuf("placed%d" % r, [P, T], F32))
+            nc.vector.memset(placed[r][:], 0.0)
+
+        pairs, picked, woven, codes, scale = {}, {}, {}, {}, {}
+        for g in range(PASSES):
+            for u in range(2):
+                pairs[g, u] = sbuf("pairs%d%d" % (g, u), [P, 2 * T], BF16)
+            for name in "ba":
+                picked[g, name] = sbuf("picked%d%s" % (g, name), [P, 2 * J], U32)
+                woven[g, name] = sbuf("woven%d%s" % (g, name), [P, 4 * J], BF16)
+                codes[g, name] = sbuf("codes%d%s" % (g, name), [P, J], U32)
+                scale[g, name] = sbuf("scale%d%s" % (g, name), [P, J], U8)
+
+        def cast(g, u, h, lo, hi, on_vector):
+            dst = pairs[g, u][:, 2 * (h * HALF_T + lo) : 2 * (h * HALF_T + hi)].rearrange("p (t e) -> p t e", e=2)
+            src = raw[g, u, h][:, :, lo:hi].rearrange("p e t -> p t e")
+            if on_vector:
+                nc.vector.tensor_copy(out=dst, in_=src)
+            else:
+                nc.scalar.activation(dst, src, COPY)
+
+        def gather(g, u, name, lo, hi):
+            window = pairs[g, u][:].bitcast(U32)
+            nc.vector.tensor_copy(
+                picked[g, name][:, u * J + lo : u * J + hi],
+                window.indirect(lists[name][:, lo // 16 : hi // 16]),
+            )
+
+        def weave(g, name, lo, hi, on_vector):
+            dtype = I32 if on_vector else U32
+            dst = woven[g, name][:, 4 * lo : 4 * hi].bitcast(dtype).rearrange("p (j u) -> p j u", u=2)
+            src = picked[g, name][:].bitcast(dtype).rearrange("p (u j) -> p j u", u=2)[:, lo:hi, :]
+            if on_vector:
+                nc.vector.tensor_copy(out=dst, in_=src)
+            else:
+                nc.scalar.copy(dst, src)
+
+        def quantise(g, name, lo, hi):
+            nc.vector.quantize_mx(
+                out=codes[g, name][:, lo:hi].bitcast(FP8X4),
+                scales=scale[g, name][:, lo:hi],
+                in_=woven[g, name][:, 4 * lo : 4 * hi],
+            )
+
+        cast(0, 0, 0, 0, 256, True)
+        cast(0, 0, 0, 256, 512, False)
+        cast(0, 0, 1, 0, 352, True)
+        cast(0, 0, 1, 352, 512, False)
+        for g, u in ((0, 0), (0, 1), (1, 0), (1, 1)):
+            if (g, u) != (0, 0):
+                for h in range(2):
+                    cast(g, u, h, 0, HALF_T, False)
+            if (g, u) != (1, 1):
+                for name in "ba":
+                    gather(g, u, name, 0, J)
+        for name in "ba":
+            weave(0, name, 0, J, False)
+
+        wa = sbuf("wa", [P, PASSES, 2 * N], U8)
+        wb = sbuf("wb", [P, PASSES, N], I32)
+        ws = sbuf("ws", [P, PASSES, N], U8)
+
+        def deal(dst, src, run):
+            nc.vector.tensor_copy(
+                out=dst.rearrange("p g (r c i) -> p g c r i", r=4, i=run),
+                in_=src.rearrange("p g (c i r) -> p g c r i", r=4, i=run),
+            )
+
+        for name in "ba":
+            gather(1, 1, name, 0, HALF_J)
+        deal(wb[:], wb_raw[:], 4)
+        deal(wa[:].bitcast(U16), wa_raw[:].bitcast(U16), 8)
+        deal(ws[:], ws_raw[:], 16)
+        for name in "ba":
+            weave(1, name, 0, HALF_J, False)
+        for name in "ba":
+            quantise(0, name, 0, J)
+        for name in "ba":
+            quantise(1, name, 0, HALF_J)
+
+        def product(name, r, bank, at, lo, width, passes=(0, 1)):
+            m = slice(r * P, (r + 1) * P)
+            cols = slice(lo, lo + width)
+            for g in passes:
+                if name == "a":
+                    w, w_scale = wa[:, g, 2 * r * P : 2 * (r + 1) * P].bitcast(FP4X4), ws[:, g, m]
+                else:
+                    w, w_scale = wb[:, g, m].bitcast(FP8X4), ws[4:P, g, m]
+                nc.tensor.matmul_mx(
+                    out=bank[:, at : at + width],
+                    lhsT=w,
+                    lhsT_scale=w_scale,
+                    rhs=codes[g, name][:, cols].bitcast(FP8X4),
+                    rhs_scale=scale[g, name][:, cols],
+                    start=(g == 0),
+                    stop=(g == PASSES - 1),
+                )
+
+        ans, gate = {}, {}
+
+        def half_products(r, h):
+            bank = psum.tile([P, J], F32, name="half%d%d" % (r, h))
+            product("b", r, bank, 0, h * HALF_J, HALF_J)
+            for s in range(2):
+                product("a", r, bank, HALF_J + s * P, h * HALF_J + s * P, P)
+            ans[r, h] = sbuf("ans%d%d" % (r, h), [P, HALF_J], F32)
+            gate[r, h] = sbuf("gate%d%d" % (r, h), [P, HALF_J], F32)
+            nc.scalar.activation(gate[r, h][:], bank[:, :HALF_J], SIGMOID)
+            nc.scalar.copy(ans[r, h][:], bank[:, HALF_J:])
+
+        whole = {(name, r): psum.tile([P, J], F32, name="whole_%s%d" % (name, r)) for name in "ba" for r in (2, 3)}
+        for name in "ba":
+            for r in (2, 3):
+                product(name, r, whole[name, r], 0, 0, J, (0,))
+
+        def whole_products(r):
+            bank_b, bank_a = whole["b", r], whole["a", r]
+            product("b", r, bank_b, 0, 0, J, (1,))
+            product("a", r, bank_a, 0, 0, J, (1,))
+            ans[r] = sbuf("ans%d" % r, [P, J], F32)
+            gate[r] = sbuf("gate%d" % r, [P, J], F32)
+            nc.scalar.activation(gate[r][:], bank_b[:], SIGMOID)
+            nc.scalar.copy(ans[r][:], bank_a[:])
+
+        def scatter(r, key, offsets):
+            nc.vector.tensor_tensor(placed[r][:].indirect(offsets), ans[key][:], gate[key][:], MULT)
+
+        n_chunks = T // CHUNK
+        y_bf = [sbuf("y_bf%d" % c, [P, 4 * CHUNK], BF16) for c in range(n_chunks)]
+        y_codes = sbuf("y_codes", [P, T], U32)
+        y_scale = sbuf("y_scale", [P, T], U8)
+        y = {(pair, h): sbuf("y%d%d" % (pair, h), [P, 2, HALF_T], F32) for pair in range(2) for h in range(2)}
+
+        def y_part(r, lo, hi):
+            h = lo // HALF_T
+            return y[r // 2, h][:, r % 2, lo - h * HALF_T : hi - h * HALF_T]
+
+        def add(r, lo, hi):
+            nc.vector.scalar_tensor_tensor(y_part(r, lo, hi), res_sb[r][:, lo:hi], 0.4, placed[r][:, lo:hi], MULT, ADD)
+
+        def store(r, lo, hi):
+            nc.sync.dma_start(out=out_rows[r, :, lo:hi], in_=y_part(r, lo, hi))
+
+        def round_pair(pair, c, on_vector):
+            dst = y_bf[c][:].rearrange("p (t r) -> p t r", r=4)[:, :, 2 * pair : 2 * pair + 2]
+            lo = (c % 2) * CHUNK
+            src = y[pair, c // 2][:, :, lo : lo + CHUNK].rearrange("p e t -> p t e")
+            if on_vector:
+                nc.vector.tensor_copy(out=dst, in_=src)
+            else:
+                nc.scalar.activation(dst, src, COPY)
+
+        cols = HALF_J // 16
+        half_products(0, 0)
+        half_products(1, 0)
+        for name in "ba":
+            gather(1, 1, name, HALF_J, J)
+        for name in "ba":
+            weave(1, name, HALF_J, J, True)
+        for name in "ba":
+            quantise(1, name, HALF_J, J)
+        half_products(0, 1)
+        half_products(1, 1)
+        whole_products(2)
+        whole_products(3)
+        scatter(0, (0, 0), list_a[:, :cols])
+        scatter(1, (1, 0), list_a[:, :cols])
+        scatter(0, (0, 1), list_a[:, cols:])
+        scatter(1, (1, 1), list_a[:, cols:])
+        for h in range(2):
+            for r in range(2):
+                add(r, h * HALF_T, (h + 1) * HALF_T)
+            nc.sync.dma_start(out=out_pairs[0, :, :, h * HALF_T : (h + 1) * HALF_T], in_=y[0, h][:])
+        for c in range(n_chunks):
+            round_pair(0, c, False)
+        scatter(2, 2, list_a[:])
+        scatter(3, 3, list_a[:])
+        for h in range(2):
+            add(2, h * HALF_T, (h + 1) * HALF_T)
+            store(2, h * HALF_T, (h + 1) * HALF_T)
+        words_out = out_1[0].rearrange("p t r -> p (t r)").bitcast(I32)
+        for c in range(n_chunks):
+            add(3, c * CHUNK, (c + 1) * CHUNK)
+            if c % 2:
+                store(3, (c - 1) * CHUNK, (c + 1) * CHUNK)
+        for c in range(n_chunks):
+            round_pair(1, c, c == n_chunks - 1)
+        for c in range(n_chunks):
+            span = slice(c * CHUNK, (c + 1) * CHUNK)
+            nc.vector.quantize_mx(out=y_codes[:, span].bitcast(FP8X4), scales=y_scale[:, span], in_=y_bf[c][:])
+            if c % 2:
+                both = slice((c - 1) * CHUNK, (c + 1) * CHUNK)
+                nc.sync.dma_start(out=words_out[:, both], in_=y_codes[:, both].bitcast(I32))
+        scale_out = out_2[0].bitcast(I32)
+        for q in range(4):
+            queue = nc.scalar if q % 2 else nc.sync
+            queue.dma_start(out=scale_out[4 * q : 4 * q + 4, :], in_=y_scale[32 * q : 32 * q + 4, :].bitcast(I32))

@@ -33,8 +33,8 @@ def tile_moe_one_expert_gates_another_pl_kernel(
         keep = ctx.enter_context(tc.tile_pool(name="keep", bufs=1))
         psum = ctx.enter_context(tc.psum_pool(name="psum", bufs=1))
 
-        def sbuf(name, shape, dtype):
-            return keep.tile(shape, dtype, name=name, align_bytes=64)
+        def sbuf(name, shape, dtype, tag=None):
+            return keep.tile(shape, dtype, name=name, tag=tag or name, align_bytes=64)
 
         list_a = sbuf("list_a", [P, J // 16], U16)
         list_b = sbuf("list_b", [P, J // 16], U16)
@@ -58,20 +58,16 @@ def tile_moe_one_expert_gates_another_pl_kernel(
             out=wb_raw[:], in_=wb_words.rearrange("g p n r -> g p (n r)").bitcast(I32).rearrange("g p w -> p g w")
         )
         ws_raw = sbuf("ws_raw", [P, PASSES, N], U8)
-        nc.vector.memset(ws_raw[:].bitcast(I32), 0)
-        for first_row, scales in ((0, wa_scales), (4, wb_scales)):
+        nc.gpsimd.memset(ws_raw[:].bitcast(I32), 0)
+        for first_row, scales, queue in ((0, wa_scales, nc.gpsimd), (4, wb_scales, nc.sync)):
             rows = scales.bitcast(I32).rearrange("g (q r) w -> q r g w", r=4)
             for q in range(4):
                 row = 32 * q + first_row
-                nc.sync.dma_start(out=ws_raw[row : row + 4].bitcast(I32), in_=rows[q])
+                queue.dma_start(out=ws_raw[row : row + 4].bitcast(I32), in_=rows[q])
 
         res_rows = res.rearrange("(p r) t -> r p t", r=4)
         out_rows = out_0.rearrange("(p r) t -> r p t", r=4)
         out_pairs = out_0.rearrange("(p u e) t -> u p e t", u=2, e=2)
-        res_sb = []
-        for r in range(4):
-            res_sb.append(sbuf("res%d" % r, [P, T], F32))
-            nc.sync.dma_start(out=res_sb[r][:], in_=res_rows[r])
 
         warm_in = sbuf("warm_in", [P, 1], F32)
         warm_out = sbuf("warm_out", [P, 1], F32)
@@ -87,10 +83,11 @@ def tile_moe_one_expert_gates_another_pl_kernel(
             for u in range(2):
                 pairs[g, u] = sbuf("pairs%d%d" % (g, u), [P, 2 * T], BF16)
             for name in "ba":
-                picked[g, name] = sbuf("picked%d%s" % (g, name), [P, 2 * J], U32)
+                picked[g, name] = sbuf("picked%d%s" % (g, name), [P, 2 * J + g * HALF_J], U32)
                 woven[g, name] = sbuf("woven%d%s" % (g, name), [P, 4 * J], BF16)
                 codes[g, name] = sbuf("codes%d%s" % (g, name), [P, J], U32)
-                scale[g, name] = sbuf("scale%d%s" % (g, name), [P, J], U8)
+                if (g, name) != (1, "a"):
+                    scale[g, name] = sbuf("scale%d%s" % (g, name), [P, J], U8)
 
         def cast(g, u, h, lo, hi, on_vector):
             dst = pairs[g, u][:, 2 * (h * HALF_T + lo) : 2 * (h * HALF_T + hi)].rearrange("p (t e) -> p t e", e=2)
@@ -107,10 +104,15 @@ def tile_moe_one_expert_gates_another_pl_kernel(
                 window.indirect(lists[name][:, lo // 16 : hi // 16]),
             )
 
+        def woven_words(g, name, lo, hi):
+            if g == 1 and lo == 0:
+                return picked[g, name][:, J + HALF_J :]
+            return woven[g, name][:, 4 * lo : 4 * hi].bitcast(U32)
+
         def weave(g, name, lo, hi, on_vector):
             dtype = I32 if on_vector else U32
-            dst = woven[g, name][:, 4 * lo : 4 * hi].bitcast(dtype).rearrange("p (j u) -> p j u", u=2)
-            src = picked[g, name][:].bitcast(dtype).rearrange("p (u j) -> p j u", u=2)[:, lo:hi, :]
+            dst = woven_words(g, name, lo, hi).bitcast(dtype).rearrange("p (j u) -> p j u", u=2)
+            src = picked[g, name][:, : 2 * J].bitcast(dtype).rearrange("p (u j) -> p j u", u=2)[:, lo:hi, :]
             if on_vector:
                 nc.vector.tensor_copy(out=dst, in_=src)
             else:
@@ -120,7 +122,7 @@ def tile_moe_one_expert_gates_another_pl_kernel(
             nc.vector.quantize_mx(
                 out=codes[g, name][:, lo:hi].bitcast(FP8X4),
                 scales=scale[g, name][:, lo:hi],
-                in_=woven[g, name][:, 4 * lo : 4 * hi],
+                in_=woven_words(g, name, lo, hi).bitcast(BF16),
             )
 
         cast(0, 0, 0, 0, 256, True)
@@ -137,6 +139,11 @@ def tile_moe_one_expert_gates_another_pl_kernel(
         for name in "ba":
             weave(0, name, 0, J, False)
 
+        res_sb = []
+        for r in range(4):
+            res_sb.append(sbuf("res%d" % r, [P, T], F32, tag="raw0%d%d" % (r // 2, r % 2)))
+            nc.sync.dma_start(out=res_sb[r][:], in_=res_rows[r])
+
         wa = sbuf("wa", [P, PASSES, 2 * N], U8)
         wb = sbuf("wb", [P, PASSES, N], I32)
         ws = sbuf("ws", [P, PASSES, N], U8)
@@ -151,11 +158,12 @@ def tile_moe_one_expert_gates_another_pl_kernel(
             gather(1, 1, name, 0, HALF_J)
         deal(wb[:], wb_raw[:], 4)
         deal(wa[:].bitcast(U16), wa_raw[:].bitcast(U16), 8)
-        deal(ws[:], ws_raw[:], 16)
         for name in "ba":
             weave(1, name, 0, HALF_J, False)
         for name in "ba":
             quantise(0, name, 0, J)
+        deal(ws[:], ws_raw[:], 16)
+        scale[1, "a"] = sbuf("scale1a", [P, J], U8, tag="ws_raw")
         for name in "ba":
             quantise(1, name, 0, HALF_J)
 
@@ -190,9 +198,6 @@ def tile_moe_one_expert_gates_another_pl_kernel(
             nc.scalar.copy(ans[r, h][:], bank[:, HALF_J:])
 
         whole = {(name, r): psum.tile([P, J], F32, name="whole_%s%d" % (name, r)) for name in "ba" for r in (2, 3)}
-        for name in "ba":
-            for r in (2, 3):
-                product(name, r, whole[name, r], 0, 0, J, (0,))
 
         def whole_products(r):
             bank_b, bank_a = whole["b", r], whole["a", r]
@@ -234,6 +239,9 @@ def tile_moe_one_expert_gates_another_pl_kernel(
         cols = HALF_J // 16
         half_products(0, 0)
         half_products(1, 0)
+        for name in "ba":
+            for r in (2, 3):
+                product(name, r, whole[name, r], 0, 0, J, (0,))
         for name in "ba":
             gather(1, 1, name, HALF_J, J)
         for name in "ba":

@@ -1,6 +1,7 @@
 from contextlib import ExitStack
 
 import concourse.mybir as mybir
+from concourse.masks import make_identity
 
 K, T, J, N = 1024, 1024, 512, 512
 FLOPS = 2 * 2 * K * N * J
@@ -23,6 +24,7 @@ PASSES = 2
 HALF_T = T // 2
 HALF_J = J // 2
 CHUNK = 256
+RES_FACTOR = 0.4
 
 
 def tile_moe_one_expert_gates_another_pl_kernel(
@@ -67,12 +69,13 @@ def tile_moe_one_expert_gates_another_pl_kernel(
 
         res_rows = res.rearrange("(p r) t -> r p t", r=4)
         out_rows = out_0.rearrange("(p r) t -> r p t", r=4)
-        out_pairs = out_0.rearrange("(p u e) t -> u p e t", u=2, e=2)
 
         warm_in = sbuf("warm_in", [P, 1], F32)
         warm_out = sbuf("warm_out", [P, 1], F32)
         nc.vector.memset(warm_in[:], 0.0)
         nc.scalar.activation(warm_out[:], warm_in[:], SIGMOID)
+        identity = sbuf("identity", [P, P], F32)
+        make_identity(nc, identity[:])
         placed = []
         for r in range(4):
             placed.append(sbuf("placed%d" % r, [P, T], F32))
@@ -195,7 +198,7 @@ def tile_moe_one_expert_gates_another_pl_kernel(
             ans[r, h] = sbuf("ans%d%d" % (r, h), [P, HALF_J], F32)
             gate[r, h] = sbuf("gate%d%d" % (r, h), [P, HALF_J], F32)
             nc.scalar.activation(gate[r, h][:], bank[:, :HALF_J], SIGMOID)
-            nc.scalar.copy(ans[r, h][:], bank[:, HALF_J:])
+            nc.scalar.activation(ans[r, h][:], bank[:, HALF_J:], COPY, scale=1.0 / RES_FACTOR)
 
         whole = {(name, r): psum.tile([P, J], F32, name="whole_%s%d" % (name, r)) for name in "ba" for r in (2, 3)}
 
@@ -206,7 +209,8 @@ def tile_moe_one_expert_gates_another_pl_kernel(
             ans[r] = sbuf("ans%d" % r, [P, J], F32)
             gate[r] = sbuf("gate%d" % r, [P, J], F32)
             nc.scalar.activation(gate[r][:], bank_b[:], SIGMOID)
-            nc.scalar.copy(ans[r][:], bank_a[:])
+            width = J if r == 2 else HALF_J
+            nc.scalar.copy(ans[r][:, :width], bank_a[:, :width])
 
         def scatter(r, key, offsets):
             nc.vector.tensor_tensor(placed[r][:].indirect(offsets), ans[key][:], gate[key][:], MULT)
@@ -222,10 +226,37 @@ def tile_moe_one_expert_gates_another_pl_kernel(
             return y[r // 2, h][:, r % 2, lo - h * HALF_T : hi - h * HALF_T]
 
         def add(r, lo, hi):
-            nc.vector.scalar_tensor_tensor(y_part(r, lo, hi), res_sb[r][:, lo:hi], 0.4, placed[r][:, lo:hi], MULT, ADD)
+            nc.vector.scalar_tensor_tensor(y_part(r, lo, hi), res_sb[r][:, lo:hi], RES_FACTOR, placed[r][:, lo:hi], MULT, ADD)
 
-        def store(r, lo, hi):
-            nc.sync.dma_start(out=out_rows[r, :, lo:hi], in_=y_part(r, lo, hi))
+        def turn(bank, source, h, first):
+            for b in range(HALF_T // P):
+                nc.tensor.matmul(
+                    bank[:, b * P : (b + 1) * P],
+                    source[:, h * HALF_T + b * P : h * HALF_T + (b + 1) * P],
+                    identity[:],
+                    start=first and b == 0,
+                    stop=not first and b == HALF_T // P - 1,
+                    is_transpose=True,
+                )
+
+        turned_banks = {}
+
+        def turn_residual(r, h, turn_bank):
+            turned_banks[r, h] = psum.tile([P, HALF_T], F32, name="turned%d%d" % (r, h), tag=turn_bank)
+            turn(turned_banks[r, h], res_sb[r], h, True)
+
+        def add_by_transposes(r, h, back_bank, y_turned):
+            turned = turned_banks[r, h]
+            turn(turned, placed[r], h, False)
+            nc.scalar.activation(y_turned, turned[:], COPY, scale=RES_FACTOR)
+            back = psum.tile([P, HALF_T], F32, name="back%d%d" % (r, h), tag=back_bank)
+            for b in range(HALF_T // P):
+                nc.tensor.transpose(back[:, b * P : (b + 1) * P], y_turned[:, b * P : (b + 1) * P], identity[:])
+            nc.scalar.copy(y_part(r, h * HALF_T, (h + 1) * HALF_T), back[:])
+            store(nc.scalar, r, h * HALF_T, (h + 1) * HALF_T)
+
+        def store(queue, r, lo, hi):
+            queue.dma_start(out=out_rows[r, :, lo:hi], in_=y_part(r, lo, hi))
 
         def round_pair(pair, c, on_vector):
             dst = y_bf[c][:].rearrange("p (t r) -> p t r", r=4)[:, :, 2 * pair : 2 * pair + 2]
@@ -252,28 +283,36 @@ def tile_moe_one_expert_gates_another_pl_kernel(
         half_products(1, 1)
         whole_products(2)
         whole_products(3)
+        turn_residual(0, 0, "half00")
+        turn_residual(0, 1, "half10")
+        turn_residual(1, 0, "whole_b2")
+        turn_residual(1, 1, "whole_a2")
         scatter(0, (0, 0), list_a[:, :cols])
         scatter(1, (1, 0), list_a[:, :cols])
         scatter(0, (0, 1), list_a[:, cols:])
         scatter(1, (1, 1), list_a[:, cols:])
-        for h in range(2):
-            for r in range(2):
-                add(r, h * HALF_T, (h + 1) * HALF_T)
-            nc.sync.dma_start(out=out_pairs[0, :, :, h * HALF_T : (h + 1) * HALF_T], in_=y[0, h][:])
+        add_by_transposes(0, 0, "half01", y_part(2, 0, HALF_T))
+        add_by_transposes(0, 1, "half11", y_part(2, HALF_T, T))
+        add_by_transposes(1, 0, "whole_b3", y_part(3, 0, HALF_T))
+        last_turned = sbuf("last_turned", [P, HALF_T], F32)
+        add_by_transposes(1, 1, "half00", last_turned[:])
+        last_ans = sbuf("last_ans", [P, HALF_J], F32, tag="last_turned")
+        nc.scalar.copy(last_ans[:], whole["a", 3][:, HALF_J:])
         for c in range(n_chunks):
             round_pair(0, c, False)
         scatter(2, 2, list_a[:])
-        scatter(3, 3, list_a[:])
+        nc.vector.tensor_tensor(placed[3][:].indirect(list_a[:, :cols]), ans[3][:, :HALF_J], gate[3][:, :HALF_J], MULT)
         for h in range(2):
             add(2, h * HALF_T, (h + 1) * HALF_T)
-            store(2, h * HALF_T, (h + 1) * HALF_T)
+            store(nc.sync, 2, h * HALF_T, (h + 1) * HALF_T)
+        nc.vector.tensor_tensor(placed[3][:].indirect(list_a[:, cols:]), last_ans[:], gate[3][:, HALF_J:], MULT)
         words_out = out_1[0].rearrange("p t r -> p (t r)").bitcast(I32)
         for c in range(n_chunks):
             add(3, c * CHUNK, (c + 1) * CHUNK)
             if c % 2:
-                store(3, (c - 1) * CHUNK, (c + 1) * CHUNK)
+                store(nc.sync, 3, (c - 1) * CHUNK, (c + 1) * CHUNK)
         for c in range(n_chunks):
-            round_pair(1, c, c == n_chunks - 1)
+            round_pair(1, c, c < n_chunks // 2)
         for c in range(n_chunks):
             span = slice(c * CHUNK, (c + 1) * CHUNK)
             nc.vector.quantize_mx(out=y_codes[:, span].bitcast(FP8X4), scales=y_scale[:, span], in_=y_bf[c][:])

@@ -42,6 +42,8 @@ def tile_moe_one_expert_gates_another_pl_kernel(
         list_b = sbuf("list_b", [P, J // 16], U16)
         lists = {"a": list_a, "b": list_b}
 
+        identity = sbuf("identity", [P, P], F32)
+        make_identity(nc, identity[:])
         x_rows = xt.rearrange("(g p u e) t -> g u p e t", g=PASSES, u=2, e=2)
         raw = {}
         for g in range(PASSES):
@@ -59,6 +61,9 @@ def tile_moe_one_expert_gates_another_pl_kernel(
         nc.sync.dma_start(
             out=wb_raw[:], in_=wb_words.rearrange("g p n r -> g p (n r)").bitcast(I32).rearrange("g p w -> p g w")
         )
+        res_rows = res.rearrange("(p r) t -> r p t", r=4)
+        res_sb = [sbuf("res0", [P, T], F32)]
+        nc.sync.dma_start(out=res_sb[0][:], in_=res_rows[0])
         ws_raw = sbuf("ws_raw", [P, PASSES, N], U8)
         nc.gpsimd.memset(ws_raw[:].bitcast(I32), 0)
         for first_row, scales, queue in ((0, wa_scales, nc.gpsimd), (4, wb_scales, nc.sync)):
@@ -67,15 +72,12 @@ def tile_moe_one_expert_gates_another_pl_kernel(
                 row = 32 * q + first_row
                 queue.dma_start(out=ws_raw[row : row + 4].bitcast(I32), in_=rows[q])
 
-        res_rows = res.rearrange("(p r) t -> r p t", r=4)
         out_rows = out_0.rearrange("(p r) t -> r p t", r=4)
 
         warm_in = sbuf("warm_in", [P, 1], F32)
         warm_out = sbuf("warm_out", [P, 1], F32)
         nc.vector.memset(warm_in[:], 0.0)
         nc.scalar.activation(warm_out[:], warm_in[:], SIGMOID)
-        identity = sbuf("identity", [P, P], F32)
-        make_identity(nc, identity[:])
         placed = []
         for r in range(4):
             placed.append(sbuf("placed%d" % r, [P, T], F32))
@@ -142,8 +144,7 @@ def tile_moe_one_expert_gates_another_pl_kernel(
         for name in "ba":
             weave(0, name, 0, J, False)
 
-        res_sb = []
-        for r in range(4):
+        for r in range(1, 4):
             res_sb.append(sbuf("res%d" % r, [P, T], F32, tag="raw0%d%d" % (r // 2, r % 2)))
             nc.sync.dma_start(out=res_sb[r][:], in_=res_rows[r])
 
@@ -200,12 +201,15 @@ def tile_moe_one_expert_gates_another_pl_kernel(
             nc.scalar.activation(gate[r, h][:], bank[:, :HALF_J], SIGMOID)
             nc.scalar.activation(ans[r, h][:], bank[:, HALF_J:], COPY, scale=1.0 / RES_FACTOR)
 
-        whole = {(name, r): psum.tile([P, J], F32, name="whole_%s%d" % (name, r)) for name in "ba" for r in (2, 3)}
+        whole = {(name, 2): psum.tile([P, J], F32, name="whole_%s2" % name) for name in "ba"}
 
-        def whole_products(r):
+        def whole_products(r, passes):
             bank_b, bank_a = whole["b", r], whole["a", r]
-            product("b", r, bank_b, 0, 0, J, (1,))
-            product("a", r, bank_a, 0, 0, J, (1,))
+            product("b", r, bank_b, 0, 0, J, passes)
+            product("a", r, bank_a, 0, 0, J, passes)
+
+        def whole_answers(r):
+            bank_b, bank_a = whole["b", r], whole["a", r]
             ans[r] = sbuf("ans%d" % r, [P, J], F32)
             gate[r] = sbuf("gate%d" % r, [P, J], F32)
             nc.scalar.activation(gate[r][:], bank_b[:], SIGMOID)
@@ -268,11 +272,12 @@ def tile_moe_one_expert_gates_another_pl_kernel(
                 nc.scalar.activation(dst, src, COPY)
 
         cols = HALF_J // 16
+        turn_residual(0, 0, "early0")
+        turn_residual(0, 1, "early1")
         half_products(0, 0)
         half_products(1, 0)
         for name in "ba":
-            for r in (2, 3):
-                product(name, r, whole[name, r], 0, 0, J, (0,))
+            product(name, 2, whole[name, 2], 0, 0, J, (0,))
         for name in "ba":
             gather(1, 1, name, HALF_J, J)
         for name in "ba":
@@ -281,23 +286,25 @@ def tile_moe_one_expert_gates_another_pl_kernel(
             quantise(1, name, HALF_J, J)
         half_products(0, 1)
         half_products(1, 1)
-        whole_products(2)
-        whole_products(3)
-        turn_residual(0, 0, "half00")
-        turn_residual(0, 1, "half10")
-        turn_residual(1, 0, "whole_b2")
-        turn_residual(1, 1, "whole_a2")
+        whole_products(2, (1,))
+        whole_answers(2)
+        whole["b", 3] = psum.tile([P, J], F32, name="whole_b3", tag="half00")
+        whole["a", 3] = psum.tile([P, J], F32, name="whole_a3", tag="half10")
+        whole_products(3, (0, 1))
+        turn_residual(1, 0, "half01")
+        turn_residual(1, 1, "half11")
         scatter(0, (0, 0), list_a[:, :cols])
         scatter(1, (1, 0), list_a[:, :cols])
         scatter(0, (0, 1), list_a[:, cols:])
         scatter(1, (1, 1), list_a[:, cols:])
-        add_by_transposes(0, 0, "half01", y_part(2, 0, HALF_T))
-        add_by_transposes(0, 1, "half11", y_part(2, HALF_T, T))
-        add_by_transposes(1, 0, "whole_b3", y_part(3, 0, HALF_T))
+        add_by_transposes(0, 0, "whole_b2", y_part(2, 0, HALF_T))
+        add_by_transposes(0, 1, "whole_a2", y_part(2, HALF_T, T))
+        whole_answers(3)
         last_turned = sbuf("last_turned", [P, HALF_T], F32)
-        add_by_transposes(1, 1, "half00", last_turned[:])
+        add_by_transposes(1, 0, "early0", last_turned[:])
         last_ans = sbuf("last_ans", [P, HALF_J], F32, tag="last_turned")
         nc.scalar.copy(last_ans[:], whole["a", 3][:, HALF_J:])
+        add_by_transposes(1, 1, "early1", y_part(3, 0, HALF_T))
         for c in range(n_chunks):
             round_pair(0, c, False)
         scatter(2, 2, list_a[:])

from contextlib import ExitStack

import concourse.mybir as mybir
from concourse.masks import make_identity

K, T, J, N = 1024, 1024, 512, 512
FLOPS = 2 * 2 * K * N * J

F32 = mybir.dt.float32
BF16 = mybir.dt.bfloat16
I32 = mybir.dt.int32
U32 = mybir.dt.uint32
U16 = mybir.dt.uint16
U8 = mybir.dt.uint8
FP8X4 = mybir.dt.float8_e4m3fn_x4
FP4X4 = mybir.dt.float4_e2m1fn_x4
COPY = mybir.ActivationFunctionType.Copy
SIGMOID = mybir.ActivationFunctionType.Sigmoid
MULT = mybir.AluOpType.mult
ADD = mybir.AluOpType.add

P = 128
PASSES = 2
HALF_T = T // 2
HALF_J = J // 2
CHUNK = 256
RES_FACTOR = 0.4


def tile_moe_one_expert_gates_another_pl_kernel(
    tc, xt, wa_words, wa_scales, wb_words, wb_scales, res, offs, offs2, out_0, out_1, out_2
):
    nc = tc.nc
    with ExitStack() as ctx:
        keep = ctx.enter_context(tc.tile_pool(name="keep", bufs=1))
        psum = ctx.enter_context(tc.psum_pool(name="psum", bufs=1))

        def sbuf(name, shape, dtype, tag=None):
            return keep.tile(shape, dtype, name=name, tag=tag or name, align_bytes=64)

        list_a = sbuf("list_a", [P, J // 16], U16)
        list_b = sbuf("list_b", [P, J // 16], U16)
        lists = {"a": list_a, "b": list_b}

        identity = sbuf("identity", [P, P], F32)
        make_identity(nc, identity[:])
        x_rows = xt.rearrange("(g p u e) t -> g u p e t", g=PASSES, u=2, e=2)
        raw = {}
        for g in range(PASSES):
            for u in range(2):
                for h in range(2):
                    raw[g, u, h] = sbuf("raw%d%d%d" % (g, u, h), [P, 2, HALF_T], F32)
                    nc.sync.dma_start(out=raw[g, u, h][:], in_=x_rows[g, u, :, :, h * HALF_T : (h + 1) * HALF_T])
                if (g, u) == (0, 0):
                    nc.sync.dma_start(list_b[:], offs2)
                    nc.sync.dma_start(list_a[:], offs)

        wa_raw = sbuf("wa_raw", [P, PASSES, 2 * N], U8)
        wb_raw = sbuf("wb_raw", [P, PASSES, N], I32)
        nc.sync.dma_start(out=wa_raw[:].bitcast(I32), in_=wa_words.bitcast(I32).rearrange("g p w -> p g w"))
        nc.sync.dma_start(
            out=wb_raw[:], in_=wb_words.rearrange("g p n r -> g p (n r)").bitcast(I32).rearrange("g p w -> p g w")
        )
        res_rows = res.rearrange("(p r) t -> r p t", r=4)
        res_sb = [sbuf("res0", [P, T], F32)]
        nc.sync.dma_start(out=res_sb[0][:], in_=res_rows[0])
        ws_raw = sbuf("ws_raw", [P, PASSES, N], U8)
        nc.gpsimd.memset(ws_raw[:].bitcast(I32), 0)
        for first_row, scales, queue in ((0, wa_scales, nc.gpsimd), (4, wb_scales, nc.sync)):
            rows = scales.bitcast(I32).rearrange("g (q r) w -> q r g w", r=4)
            for q in range(4):
                row = 32 * q + first_row
                queue.dma_start(out=ws_raw[row : row + 4].bitcast(I32), in_=rows[q])

        out_rows = out_0.rearrange("(p r) t -> r p t", r=4)

        warm_in = sbuf("warm_in", [P, 1], F32)
        warm_out = sbuf("warm_out", [P, 1], F32)
        nc.vector.memset(warm_in[:], 0.0)
        nc.scalar.activation(warm_out[:], warm_in[:], SIGMOID)
        placed = []
        for r in range(4):
            placed.append(sbuf("placed%d" % r, [P, T], F32))
            nc.vector.memset(placed[r][:], 0.0)

        pairs, picked, woven, codes, scale = {}, {}, {}, {}, {}
        for g in range(PASSES):
            for u in range(2):
                pairs[g, u] = sbuf("pairs%d%d" % (g, u), [P, 2 * T], BF16)
            for name in "ba":
                picked[g, name] = sbuf("picked%d%s" % (g, name), [P, 2 * J + g * HALF_J], U32)
                woven[g, name] = sbuf("woven%d%s" % (g, name), [P, 4 * J], BF16)
                codes[g, name] = sbuf("codes%d%s" % (g, name), [P, J], U32)
                if (g, name) != (1, "a"):
                    scale[g, name] = sbuf("scale%d%s" % (g, name), [P, J], U8)

        def cast(g, u, h, lo, hi, on_vector):
            dst = pairs[g, u][:, 2 * (h * HALF_T + lo) : 2 * (h * HALF_T + hi)].rearrange("p (t e) -> p t e", e=2)
            src = raw[g, u, h][:, :, lo:hi].rearrange("p e t -> p t e")
            if on_vector:
                nc.vector.tensor_copy(out=dst, in_=src)
            else:
                nc.scalar.activation(dst, src, COPY)

        def gather(g, u, name, lo, hi):
            window = pairs[g, u][:].bitcast(U32)
            nc.vector.tensor_copy(
                picked[g, name][:, u * J + lo : u * J + hi],
                window.indirect(lists[name][:, lo // 16 : hi // 16]),
            )

        def woven_words(g, name, lo, hi):
            if g == 1 and lo == 0:
                return picked[g, name][:, J + HALF_J :]
            return woven[g, name][:, 4 * lo : 4 * hi].bitcast(U32)

        def weave(g, name, lo, hi, on_vector):
            dtype = I32 if on_vector else U32
            dst = woven_words(g, name, lo, hi).bitcast(dtype).rearrange("p (j u) -> p j u", u=2)
            src = picked[g, name][:, : 2 * J].bitcast(dtype).rearrange("p (u j) -> p j u", u=2)[:, lo:hi, :]
            if on_vector:
                nc.vector.tensor_copy(out=dst, in_=src)
            else:
                nc.scalar.copy(dst, src)

        def quantise(g, name, lo, hi):
            nc.vector.quantize_mx(
                out=codes[g, name][:, lo:hi].bitcast(FP8X4),
                scales=scale[g, name][:, lo:hi],
                in_=woven_words(g, name, lo, hi).bitcast(BF16),
            )

        cast(0, 0, 0, 0, 256, True)
        cast(0, 0, 0, 256, 512, False)
        cast(0, 0, 1, 0, 352, True)
        cast(0, 0, 1, 352, 512, False)
        for g, u in ((0, 0), (0, 1), (1, 0), (1, 1)):
            if (g, u) != (0, 0):
                for h in range(2):
                    cast(g, u, h, 0, HALF_T, False)
            if (g, u) != (1, 1):
                for name in "ba":
                    gather(g, u, name, 0, J)
        for name in "ba":
            weave(0, name, 0, J, False)

        for r in range(1, 4):
            res_sb.append(sbuf("res%d" % r, [P, T], F32, tag="raw0%d%d" % (r // 2, r % 2)))
            nc.sync.dma_start(out=res_sb[r][:], in_=res_rows[r])

        wa = sbuf("wa", [P, PASSES, 2 * N], U8)
        wb = sbuf("wb", [P, PASSES, N], I32)
        ws = sbuf("ws", [P, PASSES, N], U8)

        def deal(dst, src, run):
            nc.vector.tensor_copy(
                out=dst.rearrange("p g (r c i) -> p g c r i", r=4, i=run),
                in_=src.rearrange("p g (c i r) -> p g c r i", r=4, i=run),
            )

        for name in "ba":
            gather(1, 1, name, 0, HALF_J)
        deal(wb[:], wb_raw[:], 4)
        deal(wa[:].bitcast(U16), wa_raw[:].bitcast(U16), 8)
        for name in "ba":
            weave(1, name, 0, HALF_J, False)
        for name in "ba":
            quantise(0, name, 0, J)
        deal(ws[:], ws_raw[:], 16)
        scale[1, "a"] = sbuf("scale1a", [P, J], U8, tag="ws_raw")
        for name in "ba":
            quantise(1, name, 0, HALF_J)

        def product(name, r, bank, at, lo, width, passes=(0, 1)):
            m = slice(r * P, (r + 1) * P)
            cols = slice(lo, lo + width)
            for g in passes:
                if name == "a":
                    w, w_scale = wa[:, g, 2 * r * P : 2 * (r + 1) * P].bitcast(FP4X4), ws[:, g, m]
                else:
                    w, w_scale = wb[:, g, m].bitcast(FP8X4), ws[4:P, g, m]
                nc.tensor.matmul_mx(
                    out=bank[:, at : at + width],
                    lhsT=w,
                    lhsT_scale=w_scale,
                    rhs=codes[g, name][:, cols].bitcast(FP8X4),
                    rhs_scale=scale[g, name][:, cols],
                    start=(g == 0),
                    stop=(g == PASSES - 1),
                )

        ans, gate = {}, {}

        def half_products(r, h):
            bank = psum.tile([P, J], F32, name="half%d%d" % (r, h))
            product("b", r, bank, 0, h * HALF_J, HALF_J)
            for s in range(2):
                product("a", r, bank, HALF_J + s * P, h * HALF_J + s * P, P)
            ans[r, h] = sbuf("ans%d%d" % (r, h), [P, HALF_J], F32)
            gate[r, h] = sbuf("gate%d%d" % (r, h), [P, HALF_J], F32)
            nc.scalar.activation(gate[r, h][:], bank[:, :HALF_J], SIGMOID)
            nc.scalar.activation(ans[r, h][:], bank[:, HALF_J:], COPY, scale=1.0 / RES_FACTOR)

        whole = {(name, 2): psum.tile([P, J], F32, name="whole_%s2" % name) for name in "ba"}

        def whole_products(r, passes):
            bank_b, bank_a = whole["b", r], whole["a", r]
            product("b", r, bank_b, 0, 0, J, passes)
            product("a", r, bank_a, 0, 0, J, passes)

        def whole_answers(r):
            bank_b, bank_a = whole["b", r], whole["a", r]
            ans[r] = sbuf("ans%d" % r, [P, J], F32)
            gate[r] = sbuf("gate%d" % r, [P, J], F32)
            nc.scalar.activation(gate[r][:], bank_b[:], SIGMOID)
            width = J if r == 2 else HALF_J
            nc.scalar.copy(ans[r][:, :width], bank_a[:, :width])

        def scatter(r, key, offsets):
            nc.vector.tensor_tensor(placed[r][:].indirect(offsets), ans[key][:], gate[key][:], MULT)

        n_chunks = T // CHUNK
        y_bf = [sbuf("y_bf%d" % c, [P, 4 * CHUNK], BF16) for c in range(n_chunks)]
        y_codes = sbuf("y_codes", [P, T], U32)
        y_scale = sbuf("y_scale", [P, T], U8)
        y = {(pair, h): sbuf("y%d%d" % (pair, h), [P, 2, HALF_T], F32) for pair in range(2) for h in range(2)}

        def y_part(r, lo, hi):
            h = lo // HALF_T
            return y[r // 2, h][:, r % 2, lo - h * HALF_T : hi - h * HALF_T]

        def add(r, lo, hi):
            nc.vector.scalar_tensor_tensor(y_part(r, lo, hi), res_sb[r][:, lo:hi], RES_FACTOR, placed[r][:, lo:hi], MULT, ADD)

        def turn(bank, source, h, first):
            for b in range(HALF_T // P):
                nc.tensor.matmul(
                    bank[:, b * P : (b + 1) * P],
                    source[:, h * HALF_T + b * P : h * HALF_T + (b + 1) * P],
                    identity[:],
                    start=first and b == 0,
                    stop=not first and b == HALF_T // P - 1,
                    is_transpose=True,
                )

        turned_banks = {}

        def turn_residual(r, h, turn_bank):
            turned_banks[r, h] = psum.tile([P, HALF_T], F32, name="turned%d%d" % (r, h), tag=turn_bank)
            turn(turned_banks[r, h], res_sb[r], h, True)

        def add_by_transposes(r, h, back_bank, y_turned):
            turned = turned_banks[r, h]
            turn(turned, placed[r], h, False)
            nc.scalar.activation(y_turned, turned[:], COPY, scale=RES_FACTOR)
            back = psum.tile([P, HALF_T], F32, name="back%d%d" % (r, h), tag=back_bank)
            for b in range(HALF_T // P):
                nc.tensor.transpose(back[:, b * P : (b + 1) * P], y_turned[:, b * P : (b + 1) * P], identity[:])
            nc.scalar.copy(y_part(r, h * HALF_T, (h + 1) * HALF_T), back[:])
            store(nc.scalar, r, h * HALF_T, (h + 1) * HALF_T)

        def store(queue, r, lo, hi):
            queue.dma_start(out=out_rows[r, :, lo:hi], in_=y_part(r, lo, hi))

        def round_pair(pair, c, on_vector):
            dst = y_bf[c][:].rearrange("p (t r) -> p t r", r=4)[:, :, 2 * pair : 2 * pair + 2]
            lo = (c % 2) * CHUNK
            src = y[pair, c // 2][:, :, lo : lo + CHUNK].rearrange("p e t -> p t e")
            if on_vector:
                nc.vector.tensor_copy(out=dst, in_=src)
            else:
                nc.scalar.activation(dst, src, COPY)

        cols = HALF_J // 16
        turn_residual(0, 0, "early0")
        turn_residual(0, 1, "early1")
        half_products(0, 0)
        half_products(1, 0)
        for name in "ba":
            product(name, 2, whole[name, 2], 0, 0, J, (0,))
        for name in "ba":
            gather(1, 1, name, HALF_J, J)
        for name in "ba":
            weave(1, name, HALF_J, J, True)
        for name in "ba":
            quantise(1, name, HALF_J, J)
        half_products(0, 1)
        half_products(1, 1)
        whole_products(2, (1,))
        whole_answers(2)
        whole["b", 3] = psum.tile([P, J], F32, name="whole_b3", tag="half00")
        whole["a", 3] = psum.tile([P, J], F32, name="whole_a3", tag="half10")
        whole_products(3, (0, 1))
        turn_residual(1, 0, "half01")
        turn_residual(1, 1, "half11")
        scatter(0, (0, 0), list_a[:, :cols])
        scatter(1, (1, 0), list_a[:, :cols])
        scatter(0, (0, 1), list_a[:, cols:])
        scatter(1, (1, 1), list_a[:, cols:])
        add_by_transposes(0, 0, "whole_b2", y_part(2, 0, HALF_T))
        add_by_transposes(0, 1, "whole_a2", y_part(2, HALF_T, T))
        whole_answers(3)
        last_turned = sbuf("last_turned", [P, HALF_T], F32)
        add_by_transposes(1, 0, "early0", last_turned[:])
        last_ans = sbuf("last_ans", [P, HALF_J], F32, tag="last_turned")
        nc.scalar.copy(last_ans[:], whole["a", 3][:, HALF_J:])
        add_by_transposes(1, 1, "early1", y_part(3, 0, HALF_T))
        for c in range(n_chunks):
            round_pair(0, c, False)
        scatter(2, 2, list_a[:])
        nc.vector.tensor_tensor(placed[3][:].indirect(list_a[:, :cols]), ans[3][:, :HALF_J], gate[3][:, :HALF_J], MULT)
        for h in range(2):
            add(2, h * HALF_T, (h + 1) * HALF_T)
            store(nc.sync, 2, h * HALF_T, (h + 1) * HALF_T)
        nc.vector.tensor_tensor(placed[3][:].indirect(list_a[:, cols:]), last_ans[:], gate[3][:, HALF_J:], MULT)
        words_out = out_1[0].rearrange("p t r -> p (t r)").bitcast(I32)
        for c in range(n_chunks):
            add(3, c * CHUNK, (c + 1) * CHUNK)
            if c % 2:
                store(nc.sync, 3, (c - 1) * CHUNK, (c + 1) * CHUNK)
        for c in range(n_chunks):
            round_pair(1, c, c < n_chunks // 2)
        for c in range(n_chunks):
            span = slice(c * CHUNK, (c + 1) * CHUNK)
            nc.vector.quantize_mx(out=y_codes[:, span].bitcast(FP8X4), scales=y_scale[:, span], in_=y_bf[c][:])
            if c % 2:
                both = slice((c - 1) * CHUNK, (c + 1) * CHUNK)
                nc.sync.dma_start(out=words_out[:, both], in_=y_codes[:, both].bitcast(I32))
        scale_out = out_2[0].bitcast(I32)
        for q in range(4):
            queue = nc.scalar if q % 2 else nc.sync
            queue.dma_start(out=scale_out[4 * q : 4 * q + 4, :], in_=y_scale[32 * q : 32 * q + 4, :].bitcast(I32))
